import numpy as np, ml_dtypes
CORES = [89,94,345,350]
N = 4
import mx_ref
NC, G, GR = 256, 2, 2
C = np.float32(0.043)
BF = ml_dtypes.bfloat16
def cut(t, i, w=512):
    return t[:, w * i:w * i + w]
def tile(rs):
    return np.stack(rs, axis=2).reshape(128, -1).astype(BF)
def layer(w, X):
    out = []
    for i in range(G):
        for t in range(len(X)):
            p = mx_ref.matmul(mx_ref.quantize(cut(w, len(X) * i + t)), X[t])
            z = p if t == 0 else z + p
        out.append(z)
    return out
def act(Z):
    return [np.maximum(s * z, 0) * C for z in Z for s in (1, -1)]
def setup_inputs(rng):
    def f(*shape):
        return mx_ref.flush((rng.standard_normal(shape, dtype=np.float32) * np.exp2(rng.integers(-2, 3, shape[:-1] + (1,)))).astype(BF))
    return {"xa": f(N, 128, 512), "xb": f(N, 128, 4 * NC), "wa": f(N, 128, G * 512), "wb": f(N, 128, G * 512)}
def setup_inputs_blocks(rng):
    d = setup_inputs(rng)
    for k in ("xa", "xb", "wa", "wb"): d[k] = mx_ref.spread(d[k], rng, 2)
    return d
def setup_inputs_wide(rng):
    d = setup_inputs(rng)
    for k in ("xa", "xb", "wa", "wb"): d[k] = mx_ref.flush((d[k].astype(np.float32) * np.exp2(rng.integers(-5, 6, (N, 1, 1))).astype(np.float32)).astype(BF))
    return d
def reference(xa, xb, wa, wb):
    A = [mx_ref.quantize(tile(act(layer(wa[j], [mx_ref.quantize(xa[j])])))) for j in range(N)]
    M = [mx_ref.quantize(tile(act(layer(wb[j], [mx_ref.quantize(xb[j])])))) for j in range(N)]
    y = np.zeros((N, 128, NC), np.float32)
    for r in range(N):
        i, j = divmod(r, GR)
        for k in range(GR):
            p = mx_ref.matmul(A[GR * i + k], M[GR * k + j])
            y[r] = p if k == 0 else y[r] + p
    return {"y": y}

@@ -1,0 +1,208 @@
+import numpy as np
+from concourse.bass import DstId, RemoteDMATransfer
+from concourse.mybir import dt, AluOpType, ActivationFunctionType
+
+X4, BF, F32 = "float8_e4m3fn_x4", "bfloat16", "float32"
+C = float(np.float32(0.043))
+GR = 2
+H = 128
+CORES_ALL = 512
+
+SCRATCH = {
+    "ixb": ("sbuf", [128, 1024], BF), "iwb": ("sbuf", [128, 1024], BF),
+    "ixa": ("sbuf", [128, 512], BF), "iwa": ("sbuf", [128, 1024], BF),
+    "qxb": ("sbuf", [128, 256], X4), "sxb": ("sbuf", [128, 256], "uint8"),
+    "qwb": ("sbuf", [128, 256], X4), "swb": ("sbuf", [128, 256], "uint8"),
+    "qxa": ("sbuf", [128, 128], X4), "sxa": ("sbuf", [128, 128], "uint8"),
+    "qwa": ("sbuf", [128, 256], X4), "swa": ("sbuf", [128, 256], "uint8"),
+    "hb": ("sbuf", [128, 1024], BF), "ha": ("sbuf", [128, 512], BF),
+    "qb": ("sbuf", [128, 256], X4), "sb": ("sbuf", [128, 256], "uint8"),
+    "qa": ("sbuf", [128, 128], X4), "sa": ("sbuf", [128, 128], "uint8"),
+    "rb": ("sbuf", [128, 256], X4), "rsb": ("sbuf", [128, 256], "uint8"),
+    "ra": ("sbuf", [128, 128], X4), "rsa": ("sbuf", [128, 128], "uint8"),
+    "oy": ("sbuf", [128, 256], F32),
+    "ps": ("psum", [128, 512 * 8], F32),
+}
+SEMAPHORES = ["lxb0", "lxb1", "lwb", "lxa", "lwa", "m0", "m1", "m2", "z00", "z10", "z01", "z11", "t0", "t1", "cb0", "cb1",
+              "ma0", "ma1", "za0", "za1", "ta", "ca", "arra", "arrb", "y0", "y1", "c0", "c1", "st", "sent", "rl0", "rl1"]
+
+
+def engines(mask):
+    return [e for e in range(mask.bit_length()) if mask >> e & 1]
+
+
+def bits(es):
+    return sum(1 << e for e in es)
+
+
+def column_partner(r):
+    return (r + GR) % (GR * GR)
+
+
+def row_partner(r):
+    return r // GR * GR + (r + 1) % GR
+
+
+def relays(T, topo):
+    out, used = {}, set(T.cores)
+    for r, s in enumerate(T.cores):
+        d = T.cores[column_partner(r)]
+        cand = [c for c in range(CORES_ALL) if topo.chip(c) == topo.chip(s) and topo.host(c) not in (topo.host(s), topo.host(d))
+                and topo.die(c) == topo.die(s) and topo.may_write(s, c) and topo.may_write(c, d) and c not in used]
+        near = [c for c in cand if topo.same_plane(s, c)][0]
+        far = [c for c in cand if topo.same_plane(c, d)][0]
+        used |= {near, far}
+        out[r] = (near, far)
+    return out
+
+
+def transfer(topo, src_core, dst_core, dst, src, es, sem):
+    rid, pid = topo.addr(dst_core, src_core)
+    return RemoteDMATransfer(dst_ids=[DstId(rid=rid, pnc=pid)], dma_engine_mask=bits(es), remote_sem=sem, src=src, dst=dst)
+
+
+def codes(t, a, b):
+    return t[:, a:b].bitcast(dt.uint8)
+
+
+def relay_program(g, core, dst_core, near, T, topo):
+    S = T.sem
+    E = engines(topo.mask(core, dst_core))
+    o = 0 if near else 64
+    first = codes(T.rb, o, o + 64)
+    g.wait_ge(S.rl0, len(E) // 2)
+    g.remote_dma_fused([transfer(topo, core, dst_core, first, first, E, S.arrb)], local_sem=S.sent)
+    second = codes(T.rb, H + o, H + o + 64)
+    g.wait_ge(S.rl1, len(E) // 2)
+    if near:
+        g.remote_dma_fused([transfer(topo, core, dst_core, second, second, E[0::2], S.arrb),
+                            transfer(topo, core, dst_core, T.rsb[:, 0:256], T.rsb[:, 0:256], E[1::2], S.arrb)], local_sem=S.sent)
+    else:
+        g.remote_dma_fused([transfer(topo, core, dst_core, second, second, E, S.arrb)], local_sem=S.sent)
+    g.wait_ge(S.sent, 2 * len(E))
+
+
+def rank_program(g, core, T, topo):
+    rank = T.rank_of(core)
+    way = relays(T, topo)
+    if rank is None:
+        for r, (near, far) in way.items():
+            if core in (near, far):
+                relay_program(g, core, T.cores[column_partner(r)], core == near, T, topo)
+        return
+
+    S = T.sem
+    Relu, Copy = ActivationFunctionType.Relu, ActivationFunctionType.Copy
+    row, col = divmod(rank, GR)
+
+    def bank(i):
+        return T.ps[:, 512 * i:512 * i + H]
+
+    g.sync.dma_start(T.iwb[:], T.wb[:]).then_inc(S.lwb, 16)
+    g.scalar.dma_start(T.ixb[:, 0:512], T.xb[:, 0:512]).then_inc(S.lxb0, 16)
+    g.scalar.dma_start(T.ixb[:, 512:1024], T.xb[:, 512:1024]).then_inc(S.lxb1, 16)
+    g.sync.dma_start(T.iwa[:], T.wa[:]).then_inc(S.lwa, 16)
+    g.scalar.dma_start(T.ixa[:], T.xa[:]).then_inc(S.lxa, 16)
+
+    def quant(q, s, a, b, src, sem):
+        g.vector.quantize_mx(q[:, a:b], s[:, a:b], src[:, 4 * a:4 * b]).then_inc(sem, 1)
+
+    def product(out, qw, sw, i, qx, sx, a, b, sem):
+        g.tensor.matmul_mx(out, qw[:, H * i:H * i + H], sw[:, H * i:H * i + H], qx[:, a:b], sx[:, a:b], True, True).then_inc(sem, 1)
+
+    def act_scalar(tile, lo, hi, z, zsem, tsem):
+        g.scalar.wait_ge(zsem, 1)
+        g.scalar.activation(tile[:, lo + 0:hi:4], z, Relu, scale=C).then_inc(tsem, 1)
+        g.scalar.activation(tile[:, lo + 1:hi:4], z, Relu, scale=-C).then_inc(tsem, 1)
+
+    def act_vector(tile, lo, hi, z, zsem, tsem):
+        g.vector.wait_ge(zsem, 1)
+        g.vector.tensor_scalar(tile[:, lo + 2:hi:4], z, C, 0.0, AluOpType.mult, AluOpType.max).then_inc(tsem, 1)
+        g.vector.tensor_scalar(tile[:, lo + 3:hi:4], z, -C, 0.0, AluOpType.mult, AluOpType.max).then_inc(tsem, 1)
+
+    v = g.vector
+    v.wait_ge(S.lxb0, 16)
+    quant(T.qxb, T.sxb, 0, H, T.ixb, S.m0)
+    v.wait_ge(S.lwb, 16)
+    quant(T.qwb, T.swb, 0, H, T.iwb, S.m0)
+    quant(T.qwb, T.swb, H, 2 * H, T.iwb, S.m1)
+    v.wait_ge(S.lxb1, 16)
+    quant(T.qxb, T.sxb, H, 2 * H, T.ixb, S.m2)
+    act_vector(T.hb, 0, 512, bank(1), S.z10, S.t0)
+    v.wait_ge(S.t0, 4)
+    quant(T.qb, T.sb, 0, H, T.hb, S.cb0)
+    act_vector(T.hb, 512, 1024, bank(3), S.z11, S.t1)
+    v.wait_ge(S.t1, 4)
+    quant(T.qb, T.sb, H, 2 * H, T.hb, S.cb1)
+    v.wait_ge(S.lxa, 16)
+    quant(T.qxa, T.sxa, 0, H, T.ixa, S.ma0)
+    v.wait_ge(S.lwa, 16)
+    quant(T.qwa, T.swa, 0, H, T.iwa, S.ma0)
+    quant(T.qwa, T.swa, H, 2 * H, T.iwa, S.ma1)
+    act_vector(T.ha, 0, 512, bank(5), S.za1, S.ta)
+    v.wait_ge(S.ta, 4)
+    quant(T.qa, T.sa, 0, H, T.ha, S.ca)
+
+    act_scalar(T.hb, 0, 512, bank(0), S.z00, S.t0)
+    act_scalar(T.hb, 512, 1024, bank(2), S.z01, S.t1)
+    act_scalar(T.ha, 0, 512, bank(4), S.za0, S.ta)
+
+    t = g.tensor
+    t.wait_ge(S.m0, 2)
+    product(bank(0), T.qwb, T.swb, 0, T.qxb, T.sxb, 0, H, S.z00)
+    t.wait_ge(S.m1, 1)
+    product(bank(1), T.qwb, T.swb, 1, T.qxb, T.sxb, 0, H, S.z10)
+    t.wait_ge(S.m2, 1)
+    product(bank(2), T.qwb, T.swb, 0, T.qxb, T.sxb, H, 2 * H, S.z01)
+    product(bank(3), T.qwb, T.swb, 1, T.qxb, T.sxb, H, 2 * H, S.z11)
+    t.wait_ge(S.ma0, 2)
+    product(bank(4), T.qwa, T.swa, 0, T.qxa, T.sxa, 0, H, S.za0)
+    t.wait_ge(S.ma1, 1)
+    product(bank(5), T.qwa, T.swa, 1, T.qxa, T.sxa, 0, H, S.za1)
+
+    near, far = way[rank]
+    E = engines(topo.mask(core, near) & topo.mask(core, far))
+    En, Ef = E[0::2], E[1::2]
+    half = len(E) // 2
+    g.wait_ge(S.cb0, 1)
+    g.remote_dma_fused([transfer(topo, core, near, codes(T.rb, 0, 64), codes(T.qb, 0, 64), En, S.rl0),
+                        transfer(topo, core, far, codes(T.rb, 64, 128), codes(T.qb, 64, 128), Ef, S.rl0)], local_sem=S.sent)
+    g.wait_ge(S.cb1, 1)
+    g.remote_dma_fused([transfer(topo, core, near, codes(T.rb, 128, 192), codes(T.qb, 128, 192), En[0::2], S.rl1),
+                        transfer(topo, core, near, T.rsb[:, 0:256], T.sb[:, 0:256], En[1::2], S.rl1),
+                        transfer(topo, core, far, codes(T.rb, 192, 256), codes(T.qb, 192, 256), Ef, S.rl1)], local_sem=S.sent)
+    mate = T.cores[row_partner(rank)]
+    rid, pid = topo.addr(mate, core)
+    A = [e for e in engines(topo.mask(core, mate)) if e not in E]
+    g.wait_ge(S.ca, 1)
+    g.remote_dma(codes(T.ra, 0, H), codes(T.qa, 0, H), S.arra, S.sent, pid, rid, bits(A))
+    g.remote_dma(T.rsa[:, 0:H], T.sa[:, 0:H], S.arra, S.sent, pid, rid, bits(A))
+
+    own_a, got_a = (T.qa, T.sa), (T.ra, T.rsa)
+    with_own_b, with_got_b = (own_a, got_a) if row == col else (got_a, own_a)
+
+    def slice_of_y(h, a, qb, sb, start, stop):
+        return t.matmul_mx(bank(6 + h), a[0][:, 0:H], a[1][:, 0:H], qb[:, H * h:H * h + H], sb[:, H * h:H * h + H], start, stop)
+
+    t.wait_ge(S.cb0, 1)
+    t.wait_ge(S.cb1, 1)
+    t.wait_ge(S.ca, 1)
+    if row != col:
+        t.wait_ge(S.arra, 2 * len(A))
+    slice_of_y(0, with_own_b, T.qb, T.sb, True, False)
+    slice_of_y(1, with_own_b, T.qb, T.sb, True, False)
+    if row == col:
+        t.wait_ge(S.arra, 2 * len(A))
+    t.wait_ge(S.arrb, 4 * len(E))
+    slice_of_y(0, with_got_b, T.rb, T.rsb, False, True).then_inc(S.y0, 1)
+    slice_of_y(1, with_got_b, T.rb, T.rsb, False, True).then_inc(S.y1, 1)
+    g.scalar.wait_ge(S.y0, 1)
+    g.scalar.activation(T.oy[:, 0:H], bank(6), Copy).then_inc(S.c0, 1)
+    g.scalar.wait_ge(S.c0, 1)
+    g.scalar.dma_start(T.y[:, 0:H], T.oy[:, 0:H]).then_inc(S.st, 16)
+    v.wait_ge(S.y1, 1)
+    v.tensor_copy(T.oy[:, H:2 * H], bank(7)).then_inc(S.c1, 1)
+    g.sync.wait_ge(S.c1, 1)
+    g.sync.dma_start(T.y[:, H:2 * H], T.oy[:, H:2 * H]).then_inc(S.st, 16)
+    g.sync.wait_ge(S.st, 32)
+    g.wait_ge(S.sent, 2 * len(E) + 2 * len(A))

@@ -68,16 +68,15 @@ def codes(t, a, b):
 def relay_program(g, core, dst_core, near, T, topo):
     S = T.sem
     E = engines(topo.mask(core, dst_core))
-    o = 0 if near else 64
-    first = codes(T.rb, o, o + 64)
+    first = codes(T.rb, 0, 32) if near else codes(T.rb, 32, 64)
     g.wait_ge(S.rl0, len(E) // 2)
     g.remote_dma_fused([transfer(topo, core, dst_core, first, first, E, S.arrb)], local_sem=S.sent)
-    second = codes(T.rb, H + o, H + o + 64)
     g.wait_ge(S.rl1, len(E) // 2)
     if near:
-        g.remote_dma_fused([transfer(topo, core, dst_core, second, second, E[0::2], S.arrb),
+        g.remote_dma_fused([transfer(topo, core, dst_core, codes(T.rb, 64, H), codes(T.rb, 64, H), E[0::2], S.arrb),
                             transfer(topo, core, dst_core, T.rsb[:, 0:256], T.rsb[:, 0:256], E[1::2], S.arrb)], local_sem=S.sent)
     else:
+        second = codes(T.rb, H, 2 * H)
         g.remote_dma_fused([transfer(topo, core, dst_core, second, second, E, S.arrb)], local_sem=S.sent)
     g.wait_ge(S.sent, 2 * len(E))
 
@@ -99,10 +98,10 @@ def rank_program(g, core, T, topo):
         return T.ps[:, 512 * i:512 * i + H]
 
     g.sync.dma_start(T.iwb[:], T.wb[:]).then_inc(S.lwb, 16)
-    g.scalar.dma_start(T.ixb[:, 0:512], T.xb[:, 0:512]).then_inc(S.lxb0, 16)
-    g.scalar.dma_start(T.ixb[:, 512:1024], T.xb[:, 512:1024]).then_inc(S.lxb1, 16)
+    g.sync.dma_start(T.ixb[:, 0:512], T.xb[:, 0:512]).then_inc(S.lxb0, 16)
+    g.sync.dma_start(T.ixb[:, 512:1024], T.xb[:, 512:1024]).then_inc(S.lxb1, 16)
+    g.sync.dma_start(T.ixa[:], T.xa[:]).then_inc(S.lxa, 16)
     g.sync.dma_start(T.iwa[:], T.wa[:]).then_inc(S.lwa, 16)
-    g.scalar.dma_start(T.ixa[:], T.xa[:]).then_inc(S.lxa, 16)
 
     def quant(q, s, a, b, src, sem):
         g.vector.quantize_mx(q[:, a:b], s[:, a:b], src[:, 4 * a:4 * b]).then_inc(sem, 1)
@@ -121,16 +120,16 @@ def rank_program(g, core, T, topo):
         g.vector.tensor_scalar(tile[:, lo + 3:hi:4], z, -C, 0.0, AluOpType.mult, AluOpType.max).then_inc(tsem, 1)
 
     v = g.vector
-    v.wait_ge(S.lxb0, 16)
-    quant(T.qxb, T.sxb, 0, H, T.ixb, S.m0)
     v.wait_ge(S.lwb, 16)
     quant(T.qwb, T.swb, 0, H, T.iwb, S.m0)
     quant(T.qwb, T.swb, H, 2 * H, T.iwb, S.m1)
-    v.wait_ge(S.lxb1, 16)
-    quant(T.qxb, T.sxb, H, 2 * H, T.ixb, S.m2)
+    v.wait_ge(S.lxb0, 16)
+    quant(T.qxb, T.sxb, 0, H, T.ixb, S.m0)
     act_vector(T.hb, 0, 512, bank(1), S.z10, S.t0)
     v.wait_ge(S.t0, 4)
     quant(T.qb, T.sb, 0, H, T.hb, S.cb0)
+    v.wait_ge(S.lxb1, 16)
+    quant(T.qxb, T.sxb, H, 2 * H, T.ixb, S.m2)
     act_vector(T.hb, 512, 1024, bank(3), S.z11, S.t1)
     v.wait_ge(S.t1, 4)
     quant(T.qb, T.sb, H, 2 * H, T.hb, S.cb1)
@@ -148,9 +147,9 @@ def rank_program(g, core, T, topo):
     act_scalar(T.ha, 0, 512, bank(4), S.za0, S.ta)
 
     t = g.tensor
+    t.wait_ge(S.m1, 1)
     t.wait_ge(S.m0, 2)
     product(bank(0), T.qwb, T.swb, 0, T.qxb, T.sxb, 0, H, S.z00)
-    t.wait_ge(S.m1, 1)
     product(bank(1), T.qwb, T.swb, 1, T.qxb, T.sxb, 0, H, S.z10)
     t.wait_ge(S.m2, 1)
     product(bank(2), T.qwb, T.swb, 0, T.qxb, T.sxb, H, 2 * H, S.z01)
@@ -163,17 +162,17 @@ def rank_program(g, core, T, topo):
     near, far = way[rank]
     E = engines(topo.mask(core, near) & topo.mask(core, far))
     En, Ef = E[0::2], E[1::2]
-    half = len(E) // 2
     g.wait_ge(S.cb0, 1)
-    g.remote_dma_fused([transfer(topo, core, near, codes(T.rb, 0, 64), codes(T.qb, 0, 64), En, S.rl0),
-                        transfer(topo, core, far, codes(T.rb, 64, 128), codes(T.qb, 64, 128), Ef, S.rl0)], local_sem=S.sent)
+    g.remote_dma_fused([transfer(topo, core, near, codes(T.rb, 0, 32), codes(T.qb, 0, 32), En, S.rl0),
+                        transfer(topo, core, far, codes(T.rb, 32, 64), codes(T.qb, 32, 64), Ef, S.rl0)], local_sem=S.sent)
     g.wait_ge(S.cb1, 1)
-    g.remote_dma_fused([transfer(topo, core, near, codes(T.rb, 128, 192), codes(T.qb, 128, 192), En[0::2], S.rl1),
+    g.remote_dma_fused([transfer(topo, core, near, codes(T.rb, 64, 128), codes(T.qb, 64, 128), En[0::2], S.rl1),
                         transfer(topo, core, near, T.rsb[:, 0:256], T.sb[:, 0:256], En[1::2], S.rl1),
-                        transfer(topo, core, far, codes(T.rb, 192, 256), codes(T.qb, 192, 256), Ef, S.rl1)], local_sem=S.sent)
+                        transfer(topo, core, far, codes(T.rb, 128, 192), codes(T.qb, 128, 192), Ef[0::2], S.rl1),
+                        transfer(topo, core, far, codes(T.rb, 192, 256), codes(T.qb, 192, 256), Ef[1::2], S.rl1)], local_sem=S.sent)
     mate = T.cores[row_partner(rank)]
     rid, pid = topo.addr(mate, core)
-    A = [e for e in engines(topo.mask(core, mate)) if e not in E]
+    A = [e for e in engines(topo.mask(core, mate)) if e not in E][0:4]
     g.wait_ge(S.ca, 1)
     g.remote_dma(codes(T.ra, 0, H), codes(T.qa, 0, H), S.arra, S.sent, pid, rid, bits(A))
     g.remote_dma(T.rsa[:, 0:H], T.sa[:, 0:H], S.arra, S.sent, pid, rid, bits(A))

@@ -8,6 +8,12 @@ GR = 2
 H = 128
 CORES_ALL = 512
 
+PIECES = [("near", "codes", 0, 48, "rl0", 0),
+          ("far", "codes", 48, 96, "rl0", 0),
+          ("plane", "plane", 0, 256, "rl0", 1),
+          ("near", "codes", 96, 176, "rl1", 1),
+          ("far", "codes", 176, 256, "rl1", 1)]
+
 SCRATCH = {
     "ixb": ("sbuf", [128, 1024], BF), "iwb": ("sbuf", [128, 1024], BF),
     "ixa": ("sbuf", [128, 512], BF), "iwa": ("sbuf", [128, 1024], BF),
@@ -23,8 +29,9 @@ SCRATCH = {
     "oy": ("sbuf", [128, 256], F32),
     "ps": ("psum", [128, 512 * 8], F32),
 }
-SEMAPHORES = ["lxb0", "lxb1", "lwb", "lxa", "lwa", "m0", "m1", "m2", "z00", "z10", "z01", "z11", "t0", "t1", "cb0", "cb1",
-              "ma0", "ma1", "za0", "za1", "ta", "ca", "arra", "arrb", "y0", "y1", "c0", "c1", "st", "sent", "rl0", "rl1"]
+SEMAPHORES = ["lxb0", "lxb1", "lwb0", "lwb1", "lxa", "lwa", "mx0", "mx1", "mw0", "mw1", "z00", "z10", "z01", "z11", "t0", "t1",
+              "cb0", "cb1", "ma0", "ma1", "za0", "za1", "ta", "ca", "arra", "arrb0", "arrb1", "y0", "y1", "c0", "c1", "st", "sent",
+              "rl0", "rl1"]
 
 
 def engines(mask):
@@ -49,45 +56,52 @@ def relays(T, topo):
         d = T.cores[column_partner(r)]
         cand = [c for c in range(CORES_ALL) if topo.chip(c) == topo.chip(s) and topo.host(c) not in (topo.host(s), topo.host(d))
                 and topo.die(c) == topo.die(s) and topo.may_write(s, c) and topo.may_write(c, d) and c not in used]
-        near = [c for c in cand if topo.same_plane(s, c)][0]
-        far = [c for c in cand if topo.same_plane(c, d)][0]
-        used |= {near, far}
-        out[r] = (near, far)
+        near = [c for c in cand if topo.same_plane(s, c)]
+        far = [c for c in cand if topo.same_plane(c, d)]
+        if r % GR:
+            near, far = near[::-1], far[::-1]
+        out[r] = {"near": near[0], "plane": near[-1], "far": far[0]}
+        used |= set(out[r].values())
     return out
-
-
-def transfer(topo, src_core, dst_core, dst, src, es, sem):
-    rid, pid = topo.addr(dst_core, src_core)
-    return RemoteDMATransfer(dst_ids=[DstId(rid=rid, pnc=pid)], dma_engine_mask=bits(es), remote_sem=sem, src=src, dst=dst)
 
 
 def codes(t, a, b):
     return t[:, a:b].bitcast(dt.uint8)
 
 
-def relay_program(g, core, dst_core, near, T, topo):
+def send(g, topo, src_core, dst_core, dst, src, es, sem, local_sem):
+    rid, pid = topo.addr(dst_core, src_core)
+    g.remote_dma_fused([RemoteDMATransfer(dst_ids=[DstId(rid=rid, pnc=pid)], dma_engine_mask=bits(es), remote_sem=sem,
+                                          src=src, dst=dst)], local_sem=local_sem)
+
+
+def piece(p, c, s):
+    return codes(c, p[2], p[3]) if p[1] == "codes" else s[:, p[2]:p[3]]
+
+
+def needed_by(p):
+    return 0 if p[2] < H else 1
+
+
+def relay_program(g, core, dst_core, way, T, topo):
     S = T.sem
     E = engines(topo.mask(core, dst_core))
-    first = codes(T.rb, 0, 32) if near else codes(T.rb, 32, 64)
-    g.wait_ge(S.rl0, len(E) // 2)
-    g.remote_dma_fused([transfer(topo, core, dst_core, first, first, E, S.arrb)], local_sem=S.sent)
-    g.wait_ge(S.rl1, len(E) // 2)
-    if near:
-        g.remote_dma_fused([transfer(topo, core, dst_core, codes(T.rb, 64, H), codes(T.rb, 64, H), E[0::2], S.arrb),
-                            transfer(topo, core, dst_core, T.rsb[:, 0:256], T.rsb[:, 0:256], E[1::2], S.arrb)], local_sem=S.sent)
-    else:
-        second = codes(T.rb, H, 2 * H)
-        g.remote_dma_fused([transfer(topo, core, dst_core, second, second, E, S.arrb)], local_sem=S.sent)
-    g.wait_ge(S.sent, 2 * len(E))
+    mine = [p for p in PIECES if p[0] == way]
+    for p in mine:
+        g.wait_ge(S[p[4]], len(E))
+        v = piece(p, T.rb, T.rsb)
+        send(g, topo, core, dst_core, v, v, E, S["arrb%d" % needed_by(p)], S.sent)
+    g.wait_ge(S.sent, len(mine) * len(E))
 
 
 def rank_program(g, core, T, topo):
     rank = T.rank_of(core)
-    way = relays(T, topo)
+    ways = relays(T, topo)
     if rank is None:
-        for r, (near, far) in way.items():
-            if core in (near, far):
-                relay_program(g, core, T.cores[column_partner(r)], core == near, T, topo)
+        for r, w in ways.items():
+            for name, c in w.items():
+                if c == core:
+                    relay_program(g, core, T.cores[column_partner(r)], name, T, topo)
         return
 
     S = T.sem
@@ -97,11 +111,12 @@ def rank_program(g, core, T, topo):
     def bank(i):
         return T.ps[:, 512 * i:512 * i + H]
 
-    g.sync.dma_start(T.iwb[:], T.wb[:]).then_inc(S.lwb, 16)
     g.sync.dma_start(T.ixb[:, 0:512], T.xb[:, 0:512]).then_inc(S.lxb0, 16)
+    g.sync.dma_start(T.iwb[:, 0:512], T.wb[:, 0:512]).then_inc(S.lwb0, 16)
+    g.sync.dma_start(T.iwb[:, 512:1024], T.wb[:, 512:1024]).then_inc(S.lwb1, 16)
     g.sync.dma_start(T.ixb[:, 512:1024], T.xb[:, 512:1024]).then_inc(S.lxb1, 16)
-    g.sync.dma_start(T.ixa[:], T.xa[:]).then_inc(S.lxa, 16)
     g.sync.dma_start(T.iwa[:], T.wa[:]).then_inc(S.lwa, 16)
+    g.sync.dma_start(T.ixa[:], T.xa[:]).then_inc(S.lxa, 16)
 
     def quant(q, s, a, b, src, sem):
         g.vector.quantize_mx(q[:, a:b], s[:, a:b], src[:, 4 * a:4 * b]).then_inc(sem, 1)
@@ -120,24 +135,25 @@ def rank_program(g, core, T, topo):
         g.vector.tensor_scalar(tile[:, lo + 3:hi:4], z, -C, 0.0, AluOpType.mult, AluOpType.max).then_inc(tsem, 1)
 
     v = g.vector
-    v.wait_ge(S.lwb, 16)
-    quant(T.qwb, T.swb, 0, H, T.iwb, S.m0)
-    quant(T.qwb, T.swb, H, 2 * H, T.iwb, S.m1)
     v.wait_ge(S.lxb0, 16)
-    quant(T.qxb, T.sxb, 0, H, T.ixb, S.m0)
+    quant(T.qxb, T.sxb, 0, H, T.ixb, S.mx0)
+    v.wait_ge(S.lwb0, 16)
+    quant(T.qwb, T.swb, 0, H, T.iwb, S.mw0)
+    v.wait_ge(S.lwb1, 16)
+    quant(T.qwb, T.swb, H, 2 * H, T.iwb, S.mw1)
     act_vector(T.hb, 0, 512, bank(1), S.z10, S.t0)
     v.wait_ge(S.t0, 4)
     quant(T.qb, T.sb, 0, H, T.hb, S.cb0)
     v.wait_ge(S.lxb1, 16)
-    quant(T.qxb, T.sxb, H, 2 * H, T.ixb, S.m2)
+    quant(T.qxb, T.sxb, H, 2 * H, T.ixb, S.mx1)
     act_vector(T.hb, 512, 1024, bank(3), S.z11, S.t1)
     v.wait_ge(S.t1, 4)
     quant(T.qb, T.sb, H, 2 * H, T.hb, S.cb1)
-    v.wait_ge(S.lxa, 16)
-    quant(T.qxa, T.sxa, 0, H, T.ixa, S.ma0)
     v.wait_ge(S.lwa, 16)
     quant(T.qwa, T.swa, 0, H, T.iwa, S.ma0)
     quant(T.qwa, T.swa, H, 2 * H, T.iwa, S.ma1)
+    v.wait_ge(S.lxa, 16)
+    quant(T.qxa, T.sxa, 0, H, T.ixa, S.ma0)
     act_vector(T.ha, 0, 512, bank(5), S.za1, S.ta)
     v.wait_ge(S.ta, 4)
     quant(T.qa, T.sa, 0, H, T.ha, S.ca)
@@ -147,11 +163,12 @@ def rank_program(g, core, T, topo):
     act_scalar(T.ha, 0, 512, bank(4), S.za0, S.ta)
 
     t = g.tensor
-    t.wait_ge(S.m1, 1)
-    t.wait_ge(S.m0, 2)
+    t.wait_ge(S.mx0, 1)
+    t.wait_ge(S.mw0, 1)
     product(bank(0), T.qwb, T.swb, 0, T.qxb, T.sxb, 0, H, S.z00)
+    t.wait_ge(S.mw1, 1)
     product(bank(1), T.qwb, T.swb, 1, T.qxb, T.sxb, 0, H, S.z10)
-    t.wait_ge(S.m2, 1)
+    t.wait_ge(S.mx1, 1)
     product(bank(2), T.qwb, T.swb, 0, T.qxb, T.sxb, H, 2 * H, S.z01)
     product(bank(3), T.qwb, T.swb, 1, T.qxb, T.sxb, H, 2 * H, S.z11)
     t.wait_ge(S.ma0, 2)
@@ -159,23 +176,19 @@ def rank_program(g, core, T, topo):
     t.wait_ge(S.ma1, 1)
     product(bank(5), T.qwa, T.swa, 1, T.qxa, T.sxa, 0, H, S.za1)
 
-    near, far = way[rank]
-    E = engines(topo.mask(core, near) & topo.mask(core, far))
-    En, Ef = E[0::2], E[1::2]
-    g.wait_ge(S.cb0, 1)
-    g.remote_dma_fused([transfer(topo, core, near, codes(T.rb, 0, 32), codes(T.qb, 0, 32), En, S.rl0),
-                        transfer(topo, core, far, codes(T.rb, 32, 64), codes(T.qb, 32, 64), Ef, S.rl0)], local_sem=S.sent)
-    g.wait_ge(S.cb1, 1)
-    g.remote_dma_fused([transfer(topo, core, near, codes(T.rb, 64, 128), codes(T.qb, 64, 128), En[0::2], S.rl1),
-                        transfer(topo, core, near, T.rsb[:, 0:256], T.sb[:, 0:256], En[1::2], S.rl1),
-                        transfer(topo, core, far, codes(T.rb, 128, 192), codes(T.qb, 128, 192), Ef[0::2], S.rl1),
-                        transfer(topo, core, far, codes(T.rb, 192, 256), codes(T.qb, 192, 256), Ef[1::2], S.rl1)], local_sem=S.sent)
+    way = ways[rank]
+    E = engines(topo.mask(core, way["near"]) & topo.mask(core, way["far"]))
+    made = -1
+    for p in PIECES:
+        if p[5] > made:
+            made = p[5]
+            g.wait_ge(S["cb%d" % made], 1)
+        send(g, topo, core, way[p[0]], piece(p, T.rb, T.rsb), piece(p, T.qb, T.sb), E, S[p[4]], S.sent)
     mate = T.cores[row_partner(rank)]
-    rid, pid = topo.addr(mate, core)
-    A = [e for e in engines(topo.mask(core, mate)) if e not in E][0:4]
+    A = [e for e in engines(topo.mask(core, mate)) if e not in E]
     g.wait_ge(S.ca, 1)
-    g.remote_dma(codes(T.ra, 0, H), codes(T.qa, 0, H), S.arra, S.sent, pid, rid, bits(A))
-    g.remote_dma(T.rsa[:, 0:H], T.sa[:, 0:H], S.arra, S.sent, pid, rid, bits(A))
+    send(g, topo, core, mate, codes(T.ra, 0, H), codes(T.qa, 0, H), A, S.arra, S.sent)
+    send(g, topo, core, mate, T.rsa[:, 0:H], T.sa[:, 0:H], A, S.arra, S.sent)
 
     own_a, got_a = (T.qa, T.sa), (T.ra, T.rsa)
     with_own_b, with_got_b = (own_a, got_a) if row == col else (got_a, own_a)
@@ -192,8 +205,9 @@ def rank_program(g, core, T, topo):
     slice_of_y(1, with_own_b, T.qb, T.sb, True, False)
     if row == col:
         t.wait_ge(S.arra, 2 * len(A))
-    t.wait_ge(S.arrb, 4 * len(E))
+    t.wait_ge(S.arrb0, len(E) * sum(needed_by(p) == 0 for p in PIECES))
     slice_of_y(0, with_got_b, T.rb, T.rsb, False, True).then_inc(S.y0, 1)
+    t.wait_ge(S.arrb1, len(E) * sum(needed_by(p) == 1 for p in PIECES))
     slice_of_y(1, with_got_b, T.rb, T.rsb, False, True).then_inc(S.y1, 1)
     g.scalar.wait_ge(S.y0, 1)
     g.scalar.activation(T.oy[:, 0:H], bank(6), Copy).then_inc(S.c0, 1)
@@ -204,4 +218,4 @@ def rank_program(g, core, T, topo):
     g.sync.wait_ge(S.c1, 1)
     g.sync.dma_start(T.y[:, H:2 * H], T.oy[:, H:2 * H]).then_inc(S.st, 16)
     g.sync.wait_ge(S.st, 32)
-    g.wait_ge(S.sent, 2 * len(E) + 2 * len(A))
+    g.wait_ge(S.sent, len(PIECES) * len(E) + 2 * len(A))

import numpy as np
from concourse.bass import DstId, RemoteDMATransfer
from concourse.mybir import dt, AluOpType, ActivationFunctionType

X4, BF, F32 = "float8_e4m3fn_x4", "bfloat16", "float32"
C = float(np.float32(0.043))
GR = 2
H = 128
CORES_ALL = 512

PIECES = [("near", "codes", 0, 48, "rl0", 0),
          ("far", "codes", 48, 96, "rl0", 0),
          ("plane", "plane", 0, 256, "rl0", 1),
          ("near", "codes", 96, 176, "rl1", 1),
          ("far", "codes", 176, 256, "rl1", 1)]

SCRATCH = {
    "ixb": ("sbuf", [128, 1024], BF), "iwb": ("sbuf", [128, 1024], BF),
    "ixa": ("sbuf", [128, 512], BF), "iwa": ("sbuf", [128, 1024], BF),
    "qxb": ("sbuf", [128, 256], X4), "sxb": ("sbuf", [128, 256], "uint8"),
    "qwb": ("sbuf", [128, 256], X4), "swb": ("sbuf", [128, 256], "uint8"),
    "qxa": ("sbuf", [128, 128], X4), "sxa": ("sbuf", [128, 128], "uint8"),
    "qwa": ("sbuf", [128, 256], X4), "swa": ("sbuf", [128, 256], "uint8"),
    "hb": ("sbuf", [128, 1024], BF), "ha": ("sbuf", [128, 512], BF),
    "qb": ("sbuf", [128, 256], X4), "sb": ("sbuf", [128, 256], "uint8"),
    "qa": ("sbuf", [128, 128], X4), "sa": ("sbuf", [128, 128], "uint8"),
    "rb": ("sbuf", [128, 256], X4), "rsb": ("sbuf", [128, 256], "uint8"),
    "ra": ("sbuf", [128, 128], X4), "rsa": ("sbuf", [128, 128], "uint8"),
    "oy": ("sbuf", [128, 256], F32),
    "ps": ("psum", [128, 512 * 8], F32),
}
SEMAPHORES = ["lxb0", "lxb1", "lwb0", "lwb1", "lxa", "lwa", "mx0", "mx1", "mw0", "mw1", "z00", "z10", "z01", "z11", "t0", "t1",
              "cb0", "cb1", "ma0", "ma1", "za0", "za1", "ta", "ca", "arra", "arrb0", "arrb1", "y0", "y1", "c0", "c1", "st", "sent",
              "rl0", "rl1"]


def engines(mask):
    return [e for e in range(mask.bit_length()) if mask >> e & 1]


def bits(es):
    return sum(1 << e for e in es)


def column_partner(r):
    return (r + GR) % (GR * GR)


def row_partner(r):
    return r // GR * GR + (r + 1) % GR


def relays(T, topo):
    out, used = {}, set(T.cores)
    for r, s in enumerate(T.cores):
        d = T.cores[column_partner(r)]
        cand = [c for c in range(CORES_ALL) if topo.chip(c) == topo.chip(s) and topo.host(c) not in (topo.host(s), topo.host(d))
                and topo.die(c) == topo.die(s) and topo.may_write(s, c) and topo.may_write(c, d) and c not in used]
        near = [c for c in cand if topo.same_plane(s, c)]
        far = [c for c in cand if topo.same_plane(c, d)]
        if r % GR:
            near, far = near[::-1], far[::-1]
        out[r] = {"near": near[0], "plane": near[-1], "far": far[0]}
        used |= set(out[r].values())
    return out


def codes(t, a, b):
    return t[:, a:b].bitcast(dt.uint8)


def send(g, topo, src_core, dst_core, dst, src, es, sem, local_sem):
    rid, pid = topo.addr(dst_core, src_core)
    g.remote_dma_fused([RemoteDMATransfer(dst_ids=[DstId(rid=rid, pnc=pid)], dma_engine_mask=bits(es), remote_sem=sem,
                                          src=src, dst=dst)], local_sem=local_sem)


def piece(p, c, s):
    return codes(c, p[2], p[3]) if p[1] == "codes" else s[:, p[2]:p[3]]


def needed_by(p):
    return 0 if p[2] < H else 1


def relay_program(g, core, dst_core, way, T, topo):
    S = T.sem
    E = engines(topo.mask(core, dst_core))
    mine = [p for p in PIECES if p[0] == way]
    for p in mine:
        g.wait_ge(S[p[4]], len(E))
        v = piece(p, T.rb, T.rsb)
        send(g, topo, core, dst_core, v, v, E, S["arrb%d" % needed_by(p)], S.sent)
    g.wait_ge(S.sent, len(mine) * len(E))


def rank_program(g, core, T, topo):
    rank = T.rank_of(core)
    ways = relays(T, topo)
    if rank is None:
        for r, w in ways.items():
            for name, c in w.items():
                if c == core:
                    relay_program(g, core, T.cores[column_partner(r)], name, T, topo)
        return

    S = T.sem
    Relu, Copy = ActivationFunctionType.Relu, ActivationFunctionType.Copy
    row, col = divmod(rank, GR)

    def bank(i):
        return T.ps[:, 512 * i:512 * i + H]

    g.sync.dma_start(T.ixb[:, 0:512], T.xb[:, 0:512]).then_inc(S.lxb0, 16)
    g.sync.dma_start(T.iwb[:, 0:512], T.wb[:, 0:512]).then_inc(S.lwb0, 16)
    g.sync.dma_start(T.iwb[:, 512:1024], T.wb[:, 512:1024]).then_inc(S.lwb1, 16)
    g.sync.dma_start(T.ixb[:, 512:1024], T.xb[:, 512:1024]).then_inc(S.lxb1, 16)
    g.sync.dma_start(T.iwa[:], T.wa[:]).then_inc(S.lwa, 16)
    g.sync.dma_start(T.ixa[:], T.xa[:]).then_inc(S.lxa, 16)

    def quant(q, s, a, b, src, sem):
        g.vector.quantize_mx(q[:, a:b], s[:, a:b], src[:, 4 * a:4 * b]).then_inc(sem, 1)

    def product(out, qw, sw, i, qx, sx, a, b, sem):
        g.tensor.matmul_mx(out, qw[:, H * i:H * i + H], sw[:, H * i:H * i + H], qx[:, a:b], sx[:, a:b], True, True).then_inc(sem, 1)

    def act_scalar(tile, lo, hi, z, zsem, tsem):
        g.scalar.wait_ge(zsem, 1)
        g.scalar.activation(tile[:, lo + 0:hi:4], z, Relu, scale=C).then_inc(tsem, 1)
        g.scalar.activation(tile[:, lo + 1:hi:4], z, Relu, scale=-C).then_inc(tsem, 1)

    def act_vector(tile, lo, hi, z, zsem, tsem):
        g.vector.wait_ge(zsem, 1)
        g.vector.tensor_scalar(tile[:, lo + 2:hi:4], z, C, 0.0, AluOpType.mult, AluOpType.max).then_inc(tsem, 1)
        g.vector.tensor_scalar(tile[:, lo + 3:hi:4], z, -C, 0.0, AluOpType.mult, AluOpType.max).then_inc(tsem, 1)

    v = g.vector
    v.wait_ge(S.lxb0, 16)
    quant(T.qxb, T.sxb, 0, H, T.ixb, S.mx0)
    v.wait_ge(S.lwb0, 16)
    quant(T.qwb, T.swb, 0, H, T.iwb, S.mw0)
    v.wait_ge(S.lwb1, 16)
    quant(T.qwb, T.swb, H, 2 * H, T.iwb, S.mw1)
    act_vector(T.hb, 0, 512, bank(1), S.z10, S.t0)
    v.wait_ge(S.t0, 4)
    quant(T.qb, T.sb, 0, H, T.hb, S.cb0)
    v.wait_ge(S.lxb1, 16)
    quant(T.qxb, T.sxb, H, 2 * H, T.ixb, S.mx1)
    act_vector(T.hb, 512, 1024, bank(3), S.z11, S.t1)
    v.wait_ge(S.t1, 4)
    quant(T.qb, T.sb, H, 2 * H, T.hb, S.cb1)
    v.wait_ge(S.lwa, 16)
    quant(T.qwa, T.swa, 0, H, T.iwa, S.ma0)
    quant(T.qwa, T.swa, H, 2 * H, T.iwa, S.ma1)
    v.wait_ge(S.lxa, 16)
    quant(T.qxa, T.sxa, 0, H, T.ixa, S.ma0)
    act_vector(T.ha, 0, 512, bank(5), S.za1, S.ta)
    v.wait_ge(S.ta, 4)
    quant(T.qa, T.sa, 0, H, T.ha, S.ca)

    act_scalar(T.hb, 0, 512, bank(0), S.z00, S.t0)
    act_scalar(T.hb, 512, 1024, bank(2), S.z01, S.t1)
    act_scalar(T.ha, 0, 512, bank(4), S.za0, S.ta)

    t = g.tensor
    t.wait_ge(S.mx0, 1)
    t.wait_ge(S.mw0, 1)
    product(bank(0), T.qwb, T.swb, 0, T.qxb, T.sxb, 0, H, S.z00)
    t.wait_ge(S.mw1, 1)
    product(bank(1), T.qwb, T.swb, 1, T.qxb, T.sxb, 0, H, S.z10)
    t.wait_ge(S.mx1, 1)
    product(bank(2), T.qwb, T.swb, 0, T.qxb, T.sxb, H, 2 * H, S.z01)
    product(bank(3), T.qwb, T.swb, 1, T.qxb, T.sxb, H, 2 * H, S.z11)
    t.wait_ge(S.ma0, 2)
    product(bank(4), T.qwa, T.swa, 0, T.qxa, T.sxa, 0, H, S.za0)
    t.wait_ge(S.ma1, 1)
    product(bank(5), T.qwa, T.swa, 1, T.qxa, T.sxa, 0, H, S.za1)

    way = ways[rank]
    E = engines(topo.mask(core, way["near"]) & topo.mask(core, way["far"]))
    made = -1
    for p in PIECES:
        if p[5] > made:
            made = p[5]
            g.wait_ge(S["cb%d" % made], 1)
        send(g, topo, core, way[p[0]], piece(p, T.rb, T.rsb), piece(p, T.qb, T.sb), E, S[p[4]], S.sent)
    mate = T.cores[row_partner(rank)]
    A = [e for e in engines(topo.mask(core, mate)) if e not in E]
    g.wait_ge(S.ca, 1)
    send(g, topo, core, mate, codes(T.ra, 0, H), codes(T.qa, 0, H), A, S.arra, S.sent)
    send(g, topo, core, mate, T.rsa[:, 0:H], T.sa[:, 0:H], A, S.arra, S.sent)

    own_a, got_a = (T.qa, T.sa), (T.ra, T.rsa)
    with_own_b, with_got_b = (own_a, got_a) if row == col else (got_a, own_a)

    def slice_of_y(h, a, qb, sb, start, stop):
        return t.matmul_mx(bank(6 + h), a[0][:, 0:H], a[1][:, 0:H], qb[:, H * h:H * h + H], sb[:, H * h:H * h + H], start, stop)

    t.wait_ge(S.cb0, 1)
    t.wait_ge(S.cb1, 1)
    t.wait_ge(S.ca, 1)
    if row != col:
        t.wait_ge(S.arra, 2 * len(A))
    slice_of_y(0, with_own_b, T.qb, T.sb, True, False)
    slice_of_y(1, with_own_b, T.qb, T.sb, True, False)
    if row == col:
        t.wait_ge(S.arra, 2 * len(A))
    t.wait_ge(S.arrb0, len(E) * sum(needed_by(p) == 0 for p in PIECES))
    slice_of_y(0, with_got_b, T.rb, T.rsb, False, True).then_inc(S.y0, 1)
    t.wait_ge(S.arrb1, len(E) * sum(needed_by(p) == 1 for p in PIECES))
    slice_of_y(1, with_got_b, T.rb, T.rsb, False, True).then_inc(S.y1, 1)
    g.scalar.wait_ge(S.y0, 1)
    g.scalar.activation(T.oy[:, 0:H], bank(6), Copy).then_inc(S.c0, 1)
    g.scalar.wait_ge(S.c0, 1)
    g.scalar.dma_start(T.y[:, 0:H], T.oy[:, 0:H]).then_inc(S.st, 16)
    v.wait_ge(S.y1, 1)
    v.tensor_copy(T.oy[:, H:2 * H], bank(7)).then_inc(S.c1, 1)
    g.sync.wait_ge(S.c1, 1)
    g.sync.dma_start(T.y[:, H:2 * H], T.oy[:, H:2 * H]).then_inc(S.st, 16)
    g.sync.wait_ge(S.st, 32)
    g.wait_ge(S.sent, len(PIECES) * len(E) + 2 * len(A))
